import numpy as np
import ml_dtypes


def mxq(x, axis, fmt="e4m3"):
    dtype, down = {"e4m3": (ml_dtypes.float8_e4m3fn, 7), "e5m2": (ml_dtypes.float8_e5m2, 14)}[fmt]
    v = np.moveaxis(np.asarray(x, np.float32).astype(ml_dtypes.bfloat16).astype(np.float64), axis, -1)
    blocks = v.reshape(v.shape[:-1] + (-1, 32))
    amax = np.abs(blocks).max(-1, keepdims=True)
    byte = np.maximum(np.where(amax > 0, np.frexp(amax)[1] - 1 + 127, 0) - down, 1)
    scale = np.exp2(byte - 127.0)
    codes = (blocks / scale).astype(np.float32).astype(dtype).astype(np.float64)
    return np.moveaxis((codes * scale).reshape(v.shape), -1, axis)


WIDE = False


def mx_kscale(k):
    if not WIDE:
        return np.ones(k)
    levels = np.array([10, -10, 5, -5, 0])
    if k % 512:
        return np.exp2(np.random.permutation(np.resize(levels, k // 32))).repeat(32)
    a = np.empty((k // 512, 16))
    for p in range(k // 512):
        a[p, :8] = np.random.permutation(np.resize(levels, 8))
        for g in range(8):
            far = levels[np.abs(levels - a[p, g]) >= 10]
            a[p, g + 8] = far[np.random.randint(len(far))]
    return np.exp2(a.ravel()).repeat(32)


BF16 = ml_dtypes.bfloat16


def bf(x):
    return np.asarray(x, np.float32).astype(BF16)


def f64(x):
    return np.asarray(x).astype(np.float64)


E2M1 = np.array([0.0, 0.5, 1.0, 1.5, 2.0, 3.0, 4.0, 6.0, -0.0, -0.5, -1.0, -1.5, -2.0, -3.0, -4.0, -6.0])


def pack_weight(w, fmt):
    k, n = w.shape
    w = f64(bf(w)).reshape(k // 32, 32, n)
    amax = np.abs(w).max(1)
    if fmt == "e4m3":
        byte = np.frexp(amax)[1] - 1 + 127 - 7
    else:
        mant, ex = np.frexp(amax / 6.0)
        byte = np.where(mant > 0.5, ex, ex - 1) + 127
    byte = np.clip(np.where(amax > 0, byte, 1), 1, 254)
    scaled = (w * np.exp2(127.0 - byte)[:, None, :]).reshape(k, n).astype(np.float32)
    by_word = np.ascontiguousarray(scaled.reshape(k // 512, 128, 4, n).transpose(0, 1, 3, 2))
    if fmt == "e4m3":
        words = by_word.astype(ml_dtypes.float8_e4m3fn).view(np.uint8)
    else:
        c = by_word.astype(ml_dtypes.float4_e2m1fn).view(np.uint8) & 0xF
        words = c[..., 0::2] | (c[..., 1::2] << 4)
    return np.ascontiguousarray(words), np.ascontiguousarray(byte.astype(np.uint8).reshape(k // 512, 16, n))


def unpack_weight(words, scales, fmt):
    g, p, n, _ = words.shape
    if fmt == "e4m3":
        vals = np.ascontiguousarray(words).view(ml_dtypes.float8_e4m3fn).astype(np.float64)
    else:
        nib = np.empty((g, p, n, 4), np.uint8)
        nib[..., 0::2] = words & 0xF
        nib[..., 1::2] = words >> 4
        vals = E2M1[nib]
    vals = vals * np.repeat(np.exp2(scales.astype(np.float64) - 127.0), 8, axis=1)[..., None]
    return vals.transpose(0, 1, 3, 2).reshape(g * 512, n)
def pack4(w):
    words, scales = pack_weight(w, "e2m1")
    return words.reshape(words.shape[0], 128, -1), scales


def unpack4(words, scales):
    return unpack_weight(words.reshape(words.shape[0], 128, -1, 2), scales, "e2m1")


def planes(Y):
    n, m = Y.shape
    b = f64(bf(Y)).reshape(n // 32, 32, m)
    amax = np.abs(b).max(1)
    byte = np.clip(np.where(amax > 0, np.frexp(amax)[1] - 1 + 127 - 7, 1), 1, 254)
    codes = (b * np.exp2(127.0 - byte)[:, None, :]).reshape(n, m).astype(np.float32).astype(ml_dtypes.float8_e4m3fn).view(np.uint8)
    words = codes.reshape(n // 512, 128, 4, m).transpose(0, 1, 3, 2)
    return np.ascontiguousarray(words), np.ascontiguousarray(byte.astype(np.uint8).reshape(n // 512, 16, m))


PROBLEMS, VARS, CONS = 1024, 1024, 2048


def setup_inputs():
    s = mx_kscale(VARS)
    t = mx_kscale(CONS)
    A = np.random.randn(CONS, VARS) / np.sqrt(VARS)
    x = np.random.randn(VARS, PROBLEMS)
    b = 0.5 * np.random.randn(PROBLEMS, CONS)
    x_words, x_scales = pack_weight(x * s[:, None], "e4m3")
    w_words, w_scales = pack4(A.T * t[None, :] / s[:, None])
    return {
        "x_words": x_words,
        "x_scales": x_scales,
        "w_words": w_words,
        "w_scales": w_scales,
        "bounds": bf(b * t[None, :]),
        "a": bf(A / t[:, None]),
        "inv_metric": bf(np.exp(0.8 * np.random.randn(VARS))),
    }

def reference(x_words, x_scales, w_words, w_scales, bounds, a, inv_metric):
    X = unpack_weight(x_words, x_scales, "e4m3")
    W = unpack4(w_words, w_scales)
    AX = X.T @ W
    R = np.maximum(AX - f64(bounds), 0.0)
    D = mxq(R, 1, "e4m3") @ mxq(f64(a), 0, "e4m3")
    y = D * f64(inv_metric)
    Y = y.T
    words, scales = planes(Y)
    return y, words, scales

from contextlib import ExitStack

import concourse.mybir as mybir
from concourse.masks import make_identity

PROBLEMS, VARS, CONS = 1024, 1024, 2048
FLOPS = 2 * 2 * PROBLEMS * VARS * CONS

F32 = mybir.dt.float32
BF16 = mybir.dt.bfloat16
I32 = mybir.dt.int32
U32 = mybir.dt.uint32
U8 = mybir.dt.uint8
FP8X4 = mybir.dt.float8_e4m3fn_x4
FP4X4 = mybir.dt.float4_e2m1fn_x4
ALU = mybir.AluOpType
ACT = mybir.ActivationFunctionType

P = 128
BANK = 512

ORDER = [
    ('msx',),
    ('ms',),
    ('D', 'w', 0),
    ('D', 'x', 0, 1),
    ('D', 'sx', 0, 0, 8),
    ('D', 'sx', 1, 0, 8),
    ('D', 'sx', 2, 0, 8),
    ('D', 'sx', 3, 0, 8),
    ('D', 'sw', 0, 0, 4),
    ('D', 'sw', 1, 0, 4),
    ('D', 'sw', 2, 0, 4),
    ('D', 'sw', 3, 0, 4),
    ('D', 'w', 1),
    ('D', 'inv'),
    ('D', 'x', 1, 2),
    ('D', 'bh', 0, 0),
    ('D', 'w', 2),
    ('D', 'w', 3),
    ('D', 'bh', 1, 0),
    ('D', 'a', 0, 0),
    ('D', 'bh', 0, 1),
    ('D', 'x', 2, 4),
    ('D', 'bh', 1, 1),
    ('D', 'b', 2),
    ('D', 'a', 1, 0),
    ('D', 'b', 3),
    ('D', 'a', 0, 1),
    ('D', 'x', 4, 8),
    ('D', 'b', 4),
    ('D', 'a', 2, 0),
    ('D', 'a', 3, 0),
    ('D', 'b', 5),
    ('D', 'a', 3, 1),
    ('D', 'b', 6),
    ('D', 'b', 7),
    ('D', 'a', 2, 1),
    ('D', 'a', 1, 1),
    ('M1', 0, 0),
    ('sub', 0, 0),
    ('M1', 0, 1),
    ('sub', 0, 1),
    ('M1', 1, 0),
    ('sub', 1, 0),
    ('M1', 1, 1),
    ('sub', 1, 1),
    ('M1', 0, 2),
    ('sub', 0, 2),
    ('M1', 0, 3),
    ('sub', 0, 3),
    ('ia', 0, 0, 0),
    ('ia', 0, 0, 1),
    ('ia', 0, 0, 2),
    ('ia', 0, 0, 3),
    ('M1', 1, 2),
    ('sub', 1, 2),
    ('M1', 1, 3),
    ('sub', 1, 3),
    ('Tinv',),
    ('cinv',),
    ('TR', 0, 0),
    ('cr', 0, 0),
    ('TR', 1, 0),
    ('cr', 1, 0),
    ('ia', 1, 0, 0),
    ('ia', 1, 0, 1),
    ('ia', 1, 0, 2),
    ('ia', 1, 0, 3),
    ('ia', 2, 0, 0),
    ('ia', 2, 0, 1),
    ('ia', 2, 0, 2),
    ('ia', 2, 0, 3),
    ('M1', 2, 0),
    ('sub', 2, 0),
    ('M1', 2, 1),
    ('sub', 2, 1),
    ('qa', 0, 0),
    ('M1', 2, 2),
    ('sub', 2, 2),
    ('M1', 2, 3),
    ('sub', 2, 3),
    ('TR', 0, 1),
    ('cr', 0, 1),
    ('TR', 1, 1),
    ('cr', 1, 1),
    ('M1', 3, 0),
    ('sub', 3, 0),
    ('M1', 3, 1),
    ('sub', 3, 1),
    ('M1', 3, 2),
    ('sub', 3, 2),
    ('M1', 3, 3),
    ('sub', 3, 3),
    ('TR', 2, 0),
    ('cr', 2, 0),
    ('TR', 2, 1),
    ('cr', 2, 1),
    ('TR', 3, 0),
    ('cr', 3, 0),
    ('ia', 0, 1, 1),
    ('qr', 0),
    ('qr', 1),
    ('qa', 1, 0),
    ('M1', 4, 0),
    ('sub', 4, 0),
    ('M1', 4, 1),
    ('sub', 4, 1),
    ('ia', 0, 1, 0),
    ('M1', 4, 2),
    ('sub', 4, 2),
    ('M1', 4, 3),
    ('sub', 4, 3),
    ('TR', 3, 1),
    ('cr', 3, 1),
    ('qr', 2),
    ('M1', 5, 0),
    ('sub', 5, 0),
    ('M1', 5, 1),
    ('sub', 5, 1),
    ('M1', 5, 2),
    ('sub', 5, 2),
    ('M1', 5, 3),
    ('sub', 5, 3),
    ('TR', 4, 0),
    ('cr', 4, 0),
    ('TR', 4, 1),
    ('cr', 4, 1),
    ('ia', 3, 0, 0),
    ('ia', 3, 0, 1),
    ('ia', 3, 0, 2),
    ('ia', 3, 0, 3),
    ('ia', 1, 1, 1),
    ('M1', 6, 0),
    ('sub', 6, 0),
    ('M1', 6, 1),
    ('sub', 6, 1),
    ('ia', 2, 1, 1),
    ('M1', 6, 2),
    ('sub', 6, 2),
    ('M1', 6, 3),
    ('sub', 6, 3),
    ('TR', 5, 0),
    ('cr', 5, 0),
    ('TR', 5, 1),
    ('cr', 5, 1),
    ('TR', 6, 0),
    ('cr', 6, 0),
    ('qa', 2, 0),
    ('qa', 3, 0),
    ('qa', 0, 1),
    ('M1', 7, 0),
    ('sub', 7, 0),
    ('M1', 7, 1),
    ('sub', 7, 1),
    ('ia', 1, 1, 0),
    ('M1', 7, 2),
    ('sub', 7, 2),
    ('M1', 7, 3),
    ('sub', 7, 3),
    ('ia', 3, 1, 1),
    ('M2', 0, 0),
    ('mul', 0, 0),
    ('sty', 0, 0),
    ('cast', 0, 0),
    ('ia', 2, 1, 0),
    ('qr', 3),
    ('qr', 4),
    ('qr', 5),
    ('M2', 1, 0),
    ('mul', 1, 0),
    ('sty', 1, 0),
    ('TR', 6, 1),
    ('cr', 6, 1),
    ('TR', 7, 0),
    ('cr', 7, 0),
    ('TR', 7, 1),
    ('cr', 7, 1),
    ('qa', 1, 1),
    ('M2', 2, 0),
    ('mul', 2, 0),
    ('sty', 2, 0),
    ('cast', 1, 0),
    ('qr', 6),
    ('M2', 3, 0),
    ('mul', 3, 0),
    ('sty', 3, 0),
    ('cast', 2, 0),
    ('qr', 7),
    ('M2', 4, 0),
    ('mul', 4, 0),
    ('sty', 4, 0),
    ('ia', 3, 1, 0),
    ('qa', 2, 1),
    ('qa', 3, 1),
    ('M2', 5, 0),
    ('mul', 5, 0),
    ('sty', 5, 0),
    ('M2', 6, 0),
    ('mul', 6, 0),
    ('sty', 6, 0),
    ('cast', 3, 0),
    ('M2', 7, 0),
    ('mul', 7, 0),
    ('sty', 7, 0),
    ('cast', 4, 0),
    ('TY', (0, 0), (1, 0)),
    ('cy', (0, 0), (1, 0)),
    ('TY', (2, 0), (3, 0)),
    ('cy', (2, 0), (3, 0)),
    ('M2', 0, 1),
    ('mul', 0, 1),
    ('sty', 0, 1),
    ('M2', 1, 1),
    ('mul', 1, 1),
    ('sty', 1, 1),
    ('cast', 6, 0),
    ('M2', 2, 1),
    ('mul', 2, 1),
    ('sty', 2, 1),
    ('cast', 0, 1),
    ('qy', (0, 0), (1, 0)),
    ('stq', (0, 0), (1, 0)),
    ('M2', 3, 1),
    ('mul', 3, 1),
    ('sty', 3, 1),
    ('cast', 5, 0),
    ('cast', 7, 0),
    ('cast', 1, 1),
    ('cast', 2, 1),
    ('TY', (4, 0), (5, 0)),
    ('cy', (4, 0), (5, 0)),
    ('TY', (6, 0), (7, 0)),
    ('cy', (6, 0), (7, 0)),
    ('TY', (0, 1), (1, 1)),
    ('cy', (0, 1), (1, 1)),
    ('qy', (2, 0), (3, 0)),
    ('stq', (2, 0), (3, 0)),
    ('qy', (4, 0), (5, 0)),
    ('stq', (4, 0), (5, 0)),
    ('qy', (6, 0), (7, 0)),
    ('stq', (6, 0), (7, 0)),
    ('sts', 0, 0),
    ('sts', 0, 1),
    ('sts', 0, 2),
    ('sts', 0, 3),
    ('M2', 4, 1),
    ('mul', 4, 1),
    ('sty', 4, 1),
    ('cast', 3, 1),
    ('M2', 5, 1),
    ('mul', 5, 1),
    ('sty', 5, 1),
    ('cast', 4, 1),
    ('M2', 6, 1),
    ('mul', 6, 1),
    ('sty', 6, 1),
    ('cast', 5, 1),
    ('TY', (2, 1), (3, 1)),
    ('cy', (2, 1), (3, 1)),
    ('qy', (0, 1), (1, 1)),
    ('stq', (0, 1), (1, 1)),
    ('qy', (2, 1), (3, 1)),
    ('stq', (2, 1), (3, 1)),
    ('M2', 7, 1),
    ('cast', 7, 1),
    ('mul', 7, 1),
    ('sty', 7, 1),
    ('cast', 6, 1),
    ('TY', (4, 1), (5, 1)),
    ('cy', (4, 1), (5, 1)),
    ('TY', (6, 1)),
    ('cy', (6, 1)),
    ('TY', (7, 1)),
    ('cy', (7, 1)),
    ('qy', (4, 1), (5, 1)),
    ('stq', (4, 1), (5, 1)),
    ('qy', (6, 1)),
    ('stq', (6, 1)),
    ('qy', (7, 1)),
    ('stq', (7, 1)),
    ('sts', 1, 0),
    ('sts', 1, 1),
    ('sts', 1, 2),
    ('sts', 1, 3),
]
RELU = ['A', 'A', 'A', 'A', 'A', 'A', 'A', 'A']
CAST = {(0, 0): 'P', (1, 0): 'P', (2, 0): 'P', (3, 0): 'P', (4, 0): 'P', (5, 0): 'P', (6, 0): 'P', (7, 0): 'P', (0, 1): 'A', (1, 1): 'A', (2, 1): 'A', (3, 1): 'A', (4, 1): 'A', (5, 1): 'A', (6, 1): 'A', (7, 1): 'B'}
ASPLIT = {(0, 0): [('POOL', 0.25), ('POOL', 0.25), ('POOL', 0.25), ('POOL', 0.25)], (0, 1): [('ACT', 0.75), ('POOL', 0.25)], (1, 0): [('POOL', 0.25), ('POOL', 0.25), ('POOL', 0.25), ('POOL', 0.25)], (1, 1): [('ACT', 0.75), ('POOL', 0.25)], (2, 0): [('POOL', 0.25), ('POOL', 0.25), ('POOL', 0.25), ('POOL', 0.25)], (2, 1): [('ACT', 0.75), ('POOL', 0.25)], (3, 0): [('POOL', 0.25), ('POOL', 0.25), ('POOL', 0.25), ('POOL', 0.25)], (3, 1): [('ACT', 0.75), ('POOL', 0.25)]}
NM = 5
LAST = (7, 1)


def tile_scaled_violation_backprojection_h2_kernel(
    tc, x_words, x_scales, w_words, w_scales, bounds, a, inv_metric, out_0, out_1, out_2
):
    nc = tc.nc
    with ExitStack() as ctx:
        keep = ctx.enter_context(tc.tile_pool(name="keep", bufs=1))
        work = ctx.enter_context(tc.tile_pool(name="work", bufs=3))
        psum = ctx.enter_context(tc.psum_pool(name="psum", bufs=1))

        xw = keep.tile([P, 2, PROBLEMS], U32, align_bytes=64)
        xs = keep.tile([P, 2, PROBLEMS], U8, align_bytes=64)
        ww = keep.tile([P, 4, 2, 2 * BANK], U8, align_bytes=64)
        ws = keep.tile([P, 2, CONS], U8, align_bytes=64)
        bnd = keep.tile([P, 8, CONS], BF16, align_bytes=64)
        araw = keep.tile([P, 8, 4, BANK], BF16, align_bytes=64)
        acode = keep.tile([P, 8, BANK], U32, align_bytes=64)
        ascale = keep.tile([P, 8, BANK], U8, align_bytes=64)
        rcode = keep.tile([P, 8, BANK], U32, align_bytes=64)
        rscale = keep.tile([P, 8, BANK], U8, align_bytes=64)
        ycode = keep.tile([P, 2, PROBLEMS], U32, align_bytes=64)
        yscale = keep.tile([P, 2, PROBLEMS], U8, align_bytes=64)
        inv_rows = keep.tile([P, 8], BF16, align_bytes=64)
        inv_all = keep.tile([P, VARS], BF16, align_bytes=64)
        ident = keep.tile([P, P], F32, align_bytes=64)

        x_src = x_words.rearrange("g p n t -> p g (n t)").bitcast(I32)
        w_src = w_words.rearrange("g p b -> p g b").bitcast(I32)
        code_dst = out_1.rearrange("g p m t -> p g (m t)").bitcast(I32)
        held = {}

        def load(kind, *ix):
            if kind == "x":
                cols = slice(ix[0] * P, ix[1] * P)
                nc.sync.dma_start(out=xw[:, :, cols].bitcast(I32), in_=x_src[:, :, cols])
            elif kind == "w":
                c = ix[0]
                nc.sync.dma_start(out=ww[:, c, :, :].bitcast(I32), in_=w_src[:, :, 256 * c : 256 * (c + 1)])
            elif kind == "inv":
                nc.sync.dma_start(out=inv_rows[:], in_=inv_metric.rearrange("(p c) -> p c", c=8))
            elif kind == "sx" or kind == "sw":
                q = ix[0]
                plane, rows = (xs, x_scales) if kind == "sx" else (ws, w_scales)
                nc.sync.dma_start(
                    out=plane[32 * q : 32 * q + 4, :, :].bitcast(I32),
                    in_=rows[:, 4 * q : 4 * q + 4, :].rearrange("g r n -> r g n").bitcast(I32),
                )
            elif kind == "bc":
                i, c = ix
                cols = slice(c * BANK, (c + 1) * BANK)
                nc.sync.dma_start(out=bnd[:, i, cols], in_=bounds[i * P : (i + 1) * P, cols])
            elif kind == "bh":
                i, j = ix
                cols = slice(j * 2 * BANK, (j + 1) * 2 * BANK)
                nc.sync.dma_start(out=bnd[:, i, cols], in_=bounds[i * P : (i + 1) * P, cols])
            elif kind == "b":
                i = ix[0]
                nc.sync.dma_start(out=bnd[:, i, :], in_=bounds[i * P : (i + 1) * P, :])
            else:
                g, h = ix
                rows = a[g * BANK : (g + 1) * BANK, h * BANK : (h + 1) * BANK]
                nc.sync.dma_start(out=araw[:, 2 * g + h, :, :], in_=rows.rearrange("(p j) v -> p j v", j=4))

        def mm_bank():
            return psum.tile([P, BANK], F32, name="mm", bufs=NM)

        def tr_bank():
            return psum.tile([P, BANK], F32, name="tr", bufs=8 - NM)

        def step(kind, *ix):
            if kind == "D":
                load(*ix)
            elif kind == "msx":
                nc.vector.memset(xs[:].rearrange("p g n -> p (g n)").bitcast(I32), 0)
            elif kind == "ms":
                nc.vector.memset(ws[:].rearrange("p g n -> p (g n)").bitcast(I32), 0)
                nc.vector.memset(ident[:], 0.0)
                make_identity(nc, ident[:], nomemset=True)

            elif kind == "Tinv":
                bank = tr_bank()
                held["inv"] = bank
                words = inv_rows[:].bitcast(F32)
                for c in range(4):
                    nc.tensor.transpose(bank[:, c * P : (c + 1) * P], words[:, c : c + 1].to_broadcast([P, P]), ident[:])
            elif kind == "cinv":
                nc.scalar.copy(
                    out=inv_all[:].bitcast(F32).rearrange("p (m c) -> p m c", c=4),
                    in_=held["inv"][:].rearrange("p (c m) -> p m c", c=4),
                )
            elif kind == "M1":
                i, c = ix
                bank = mm_bank()
                held["M1", i, c] = bank
                rows = slice(i * P, (i + 1) * P)
                for g in range(2):
                    nc.tensor.matmul_mx(
                        out=bank[:],
                        lhsT=xw[:, g, rows].bitcast(FP8X4),
                        lhsT_scale=xs[:, g, rows],
                        rhs=ww[:, c, g, :].bitcast(FP4X4),
                        rhs_scale=ws[:, g, c * BANK : (c + 1) * BANK],
                        start=(g == 0),
                        stop=(g == 1),
                    )
            elif kind == "sub":
                i, c = ix
                if c % 2 == 0:
                    held["rb", i, c // 2] = work.tile([P, 2, BANK], BF16, name="rb", bufs=5, align_bytes=64)
                nc.vector.tensor_tensor(
                    out=held["rb", i, c // 2][:, c % 2, :].rearrange("p (u m e) -> p u m e", u=2, e=2),
                    in0=held["M1", i, c][:].rearrange("p (m u e) -> p u m e", u=2, e=2),
                    in1=bnd[:, i, c * BANK : (c + 1) * BANK].rearrange("p (m u e) -> p u m e", u=2, e=2),
                    op=ALU.subtract,
                )
            elif kind == "TR":
                i, j = ix
                bank = tr_bank()
                held["TR", i, j] = bank
                words = held["rb", i, j][:].rearrange("p s k -> p (s k)").bitcast(F32)
                for s in range(2):
                    for u in range(2):
                        nc.tensor.transpose(
                            bank[:, (2 * u + s) * P : (2 * u + s + 1) * P],
                            words[:, (2 * s + u) * P : (2 * s + u + 1) * P],
                            ident[:],
                        )
            elif kind == "cr":
                i, j = ix
                if ("rq", i) not in held:
                    held["rq", i] = work.tile([P, CONS], BF16, name="rq", bufs=6, align_bytes=64)
                dst = held["rq", i][:, j * 2 * BANK : (j + 1) * 2 * BANK]
                bank = held["TR", i, j]
                if RELU[i] == "A":
                    nc.scalar.activation(
                        out=dst.rearrange("p (q u e) -> p q u e", u=2, e=2),
                        in_=bank[:].bitcast(BF16).rearrange("p (u q e) -> p q u e", u=2, e=2),
                        func=ACT.Relu,
                    )
                else:
                    nc.scalar.copy(
                        out=dst.bitcast(F32).rearrange("p (q u) -> p q u", u=2),
                        in_=bank[:].rearrange("p (u q) -> p q u", u=2),
                    )
            elif kind == "rl":
                t = held["rq", ix[0]]
                nc.vector.tensor_scalar(out=t[:], in0=t[:], scalar1=0.0, scalar2=None, op0=ALU.max)
            elif kind == "qr":
                i = ix[0]
                nc.vector.quantize_mx(out=rcode[:, i, :].bitcast(FP8X4), scales=rscale[:, i, :], in_=held["rq", i][:])
            elif kind == "ia":
                g, h, n = ix
                if ("ai", g, h) not in held:
                    held["ai", g, h] = work.tile([P, BANK, 4], BF16, name="ai", bufs=4, align_bytes=64)
                parts = ASPLIT[g, h]
                v0 = int(BANK * sum(f for e, f in parts[:n]))
                cols = slice(v0, v0 + int(BANK * parts[n][1]))
                dst = held["ai", g, h][:, cols, :] if parts[n][0] == "POOL" else held["ai", g, h][:, cols, :].rearrange("p (c i) t -> p c t i", i=4)
                src = araw[:, 2 * g + h, :, cols].rearrange("p t v -> p v t" if parts[n][0] == "POOL" else "p t (c i) -> p c t i", **({} if parts[n][0] == "POOL" else {"i": 4}))
                if parts[n][0] == "ACT":
                    nc.scalar.copy(out=dst, in_=src)
                elif parts[n][0] == "DVE":
                    nc.vector.tensor_copy(out=dst, in_=src)
                else:
                    nc.gpsimd.tensor_scalar(out=dst, in0=src, scalar1=1.0, scalar2=1.0, op0=ALU.mult, op1=ALU.mult)
            elif kind == "qa":
                g, h = ix
                nc.vector.quantize_mx(
                    out=acode[:, 2 * g + h, :].bitcast(FP8X4),
                    scales=ascale[:, 2 * g + h, :],
                    in_=held["ai", g, h][:].rearrange("p v t -> p (v t)"),
                )
            elif kind == "M2" and ix == LAST:
                i, h = ix
                for k in range(2):
                    bank = mm_bank()
                    held["M2", i, h, k] = bank
                    half = slice(k * 256, (k + 1) * 256)
                    for g in range(4):
                        cols = slice(g * P, (g + 1) * P)
                        nc.tensor.matmul_mx(
                            out=bank[:, :256],
                            lhsT=rcode[:, i, cols].bitcast(FP8X4),
                            lhsT_scale=rscale[:, i, cols],
                            rhs=acode[:, 2 * g + h, half].bitcast(FP8X4),
                            rhs_scale=ascale[:, 2 * g + h, half],
                            start=(g == 0),
                            stop=(g == 3),
                        )
            elif kind == "cast" and ix == LAST:
                i, h = ix
                yb = work.tile([P, BANK], BF16, name="yb", bufs=8, align_bytes=64)
                held["yb", i, h] = yb
                held["y", i, h] = work.tile([P, BANK], F32, name="y", bufs=8, align_bytes=64)
                for k in range(2):
                    factor = inv_all[:, h * BANK + k * 256 : h * BANK + (k + 1) * 256]
                    nc.vector.tensor_tensor(
                        out=yb[:].rearrange("p (u m e) -> p u m e", u=2, e=2)[:, :, 64 * k : 64 * (k + 1), :],
                        in0=held["M2", i, h, k][:, :256].rearrange("p (m u e) -> p u m e", u=2, e=2),
                        in1=factor.rearrange("p (m u e) -> p u m e", u=2, e=2),
                        op=ALU.mult,
                    )
                    if k == 0:
                        nc.vector.tensor_tensor(
                            out=held["y", i, h][:, :256], in0=held["M2", i, h, k][:, :256], in1=factor, op=ALU.mult
                        )
            elif kind == "mul" and ix == LAST:
                i, h = ix
                nc.vector.tensor_tensor(
                    out=held["y", i, h][:, 256:],
                    in0=held["M2", i, h, 1][:, :256],
                    in1=inv_all[:, h * BANK + 256 : (h + 1) * BANK],
                    op=ALU.mult,
                )
            elif kind == "M2":
                i, h = ix
                bank = mm_bank()
                held["M2", i, h] = bank
                for g in range(4):
                    cols = slice(g * P, (g + 1) * P)
                    nc.tensor.matmul_mx(
                        out=bank[:],
                        lhsT=rcode[:, i, cols].bitcast(FP8X4),
                        lhsT_scale=rscale[:, i, cols],
                        rhs=acode[:, 2 * g + h, :].bitcast(FP8X4),
                        rhs_scale=ascale[:, 2 * g + h, :],
                        start=(g == 0),
                        stop=(g == 3),
                    )
            elif kind == "mul":
                i, h = ix
                held["y", i, h] = work.tile([P, BANK], F32, name="y", bufs=8, align_bytes=64)
                nc.vector.tensor_tensor(
                    out=held["y", i, h][:],
                    in0=held["M2", i, h][:],
                    in1=inv_all[:, h * BANK : (h + 1) * BANK],
                    op=ALU.mult,
                )
            elif kind == "sty":
                i, h = ix
                nc.sync.dma_start(out=out_0[i * P : (i + 1) * P, h * BANK : (h + 1) * BANK], in_=held["y", i, h][:])
            elif kind == "cast":
                i, h = ix
                yb = work.tile([P, BANK], BF16, name="yb", bufs=8, align_bytes=64)
                held["yb", i, h] = yb
                dst = yb[:].rearrange("p (u m e) -> p u m e", u=2, e=2)
                if CAST[i, h] == "B":
                    nc.vector.tensor_tensor(
                        out=dst,
                        in0=held["M2", i, h][:].rearrange("p (m u e) -> p u m e", u=2, e=2),
                        in1=inv_all[:, h * BANK : (h + 1) * BANK].rearrange("p (m u e) -> p u m e", u=2, e=2),
                        op=ALU.mult,
                    )
                elif CAST[i, h] == "P":
                    nc.gpsimd.tensor_scalar(
                        out=dst,
                        in0=held["y", i, h][:].rearrange("p (m u e) -> p u m e", u=2, e=2),
                        scalar1=1.0,
                        scalar2=1.0,
                        op0=ALU.mult,
                        op1=ALU.mult,
                    )
                elif CAST[i, h] == "A":
                    nc.scalar.copy(out=dst, in_=held["y", i, h][:].rearrange("p (m u e) -> p u m e", u=2, e=2))
                else:
                    nc.vector.tensor_copy(out=dst, in_=held["y", i, h][:].rearrange("p (m u e) -> p u m e", u=2, e=2))
            elif kind == "TY":
                bank = tr_bank()
                held["TY", ix] = bank
                for s, (i, h) in enumerate(ix):
                    words = held["yb", i, h][:].bitcast(F32)
                    for u in range(2):
                        at = (len(ix) * u + s) * P
                        nc.tensor.transpose(bank[:, at : at + P], words[:, u * P : (u + 1) * P], ident[:])
            elif kind == "cy":
                width = len(ix) * P
                yq = work.tile([P, 4 * width], BF16, name="yq", bufs=4, align_bytes=64)
                held["yq", ix] = yq
                nc.scalar.copy(
                    out=yq[:].bitcast(F32).rearrange("p (q u) -> p q u", u=2),
                    in_=held["TY", ix][:, : 2 * width].rearrange("p (u q) -> p q u", u=2),
                )
            elif kind == "qy":
                i, h = ix[0]
                cols = slice(i * P, (i + len(ix)) * P)
                nc.vector.quantize_mx(
                    out=ycode[:, h, cols].bitcast(FP8X4), scales=yscale[:, h, cols], in_=held["yq", ix][:]
                )
            elif kind == "stq":
                i, h = ix[0]
                cols = slice(i * P, (i + len(ix)) * P)
                nc.sync.dma_start(out=code_dst[:, h, cols], in_=ycode[:, h, cols].bitcast(I32))
            else:
                h, q = ix
                queue = nc.scalar if h == 1 and q >= 2 else nc.sync
                queue.dma_start(
                    out=out_2[h, 4 * q : 4 * q + 4, :].bitcast(I32),
                    in_=yscale[32 * q : 32 * q + 4, h, :].bitcast(I32),
                )

        with tc.manual_schedule():
            for task in ORDER:
                step(*task)
